import numpy as np
import ml_dtypes


def mxq(x, axis, fmt="e4m3"):
    dtype, down = {"e4m3": (ml_dtypes.float8_e4m3fn, 7), "e5m2": (ml_dtypes.float8_e5m2, 14)}[fmt]
    v = np.moveaxis(np.asarray(x, np.float32).astype(ml_dtypes.bfloat16).astype(np.float64), axis, -1)
    blocks = v.reshape(v.shape[:-1] + (-1, 32))
    amax = np.abs(blocks).max(-1, keepdims=True)
    byte = np.maximum(np.where(amax > 0, np.frexp(amax)[1] - 1 + 127, 0) - down, 1)
    scale = np.exp2(byte - 127.0)
    codes = (blocks / scale).astype(np.float32).astype(dtype).astype(np.float64)
    return np.moveaxis((codes * scale).reshape(v.shape), -1, axis)


WIDE = False


def mx_kscale(k):
    if not WIDE:
        return np.ones(k)
    levels = np.array([10, -10, 5, -5, 0])
    if k % 512:
        return np.exp2(np.random.permutation(np.resize(levels, k // 32))).repeat(32)
    a = np.empty((k // 512, 16))
    for p in range(k // 512):
        a[p, :8] = np.random.permutation(np.resize(levels, 8))
        for g in range(8):
            far = levels[np.abs(levels - a[p, g]) >= 10]
            a[p, g + 8] = far[np.random.randint(len(far))]
    return np.exp2(a.ravel()).repeat(32)


BF16 = ml_dtypes.bfloat16


def bf(x):
    return np.asarray(x, np.float32).astype(BF16)


def f64(x):
    return np.asarray(x).astype(np.float64)


T, D, F, R, E = 128, 2048, 4096, 128, 16
ER = E * R


def draw0():
    u = mx_kscale(D)
    t = mx_kscale(ER)
    return {"x": bf(np.random.standard_normal((T, D)) * u),
            "w0": bf(np.random.standard_normal((D, F)) / np.sqrt(D) / u[:, None]),
            "wa": bf(np.random.standard_normal((D, R)) / np.sqrt(D) / u[:, None]),
            "c": bf(np.random.standard_normal((E, R))),
            "s": bf((1.0 + 0.1 * np.random.standard_normal(ER)) * t),
            "wb": bf(np.random.standard_normal((ER, F)) / np.sqrt(R) / t[:, None])}


def prototype_gate(a, c):
    diff = a[:, None, :] - c[None, :, :]
    logits = -np.sum(diff * diff, axis=-1) / 16.0
    e = np.exp(logits - logits.max(-1, keepdims=True))
    return e / e.sum(-1, keepdims=True)


def core(x, w0, wa, c, s, wb):
    xq = mxq(f64(x), 1, "e4m3")
    a = xq @ mxq(f64(wa), 0, "e4m3")
    g = prototype_gate(a, f64(c))
    z = (g[:, :, None] * a[:, None, :]).reshape(x.shape[0], wb.shape[0])
    zs = z * f64(s)[None, :]
    low = mxq(zs, 1, "e4m3") @ mxq(f64(wb), 0, "e4m3")
    return (xq @ mxq(f64(w0), 0, "e4m3")) + 1.5 * low


def e4m3fn_bytes(y):
    return np.clip(np.asarray(y, np.float64), -448.0, 448.0).astype(np.float32).astype(ml_dtypes.float8_e4m3fn).view(np.uint8)


def e4m3fn_values(b):
    return np.asarray(b, np.uint8).view(ml_dtypes.float8_e4m3fn).astype(np.float64)


def setup_inputs():
    d = draw0()
    x0 = np.asarray(d['wb']).astype(np.float64)
    s = (np.max(np.abs(x0), axis=(1,), keepdims=True) / 448.0).astype(np.float32)
    out = {}
    for k, v in d.items():
        if k == 'wb':
            out['wb_bytes'] = e4m3fn_bytes(x0 / s.astype(np.float64))
            out['wb_scale'] = s
        else:
            out[k] = v
    return out


def reference(x, w0, wa, c, s, wb_bytes, wb_scale):
    return core(x, w0, wa, c, s, e4m3fn_values(wb_bytes) * wb_scale.astype(np.float64))

@@ -1,0 +1,306 @@
+from contextlib import ExitStack
+
+import concourse.mybir as mybir
+from concourse.masks import make_identity
+
+T, D, F, R, E = 128, 2048, 4096, 128, 16
+FLOPS = 2 * T * D * F * 2 + 2 * T * D * R
+
+F32 = mybir.dt.float32
+BF16 = mybir.dt.bfloat16
+U32 = mybir.dt.uint32
+U8 = mybir.dt.uint8
+F8 = mybir.dt.float8_e4m3fn
+X4 = mybir.dt.float8_e4m3fn_x4
+ACT = mybir.ActivationFunctionType
+ALU = mybir.AluOpType
+AX = mybir.AxisListType
+
+P = 128
+PACK = 4
+G = 4
+BANK = 512
+CHUNKS = [256,512,1024,1024,1024,256]
+S_SHARE = 6
+
+
+def tile_hydraloraprototyperouted_w_kernel(tc, x, w0, wa, c, s, wb_bytes, wb_scale, out):
+    nc = tc.nc
+    with ExitStack() as ctx:
+        keep = ctx.enter_context(tc.tile_pool(name="keep", bufs=1))
+        stream = ctx.enter_context(tc.tile_pool(name="stream", bufs=3))
+        psum = ctx.enter_context(tc.psum_pool(name="psum", bufs=1))
+        ctx.enter_context(tc.manual_schedule())
+
+        steps = []
+        n0 = 0
+        for ci, w in enumerate(CHUNKS):
+            for g in range(G):
+                steps.append((ci, g, n0, w))
+            n0 += w
+        n = len(steps)
+        st = [dict() for i in range(n)]
+        acc = {}
+        count = {}
+
+        def load_w(i):
+            if not 0 <= i < n:
+                return
+            ci, g, n0, w = steps[i]
+            t = stream.tile([P, PACK, w], BF16, name="w_raw", bufs=5)
+            nc.sync.dma_start(out=t[:], in_=w0[g * 512:(g + 1) * 512, n0:n0 + w].rearrange("(p j) n -> p j n", j=PACK))
+            st[i]["w_raw"] = t
+
+        def load_b(i):
+            if not 0 <= i < n:
+                return
+            ci, g, n0, w = steps[i]
+            t = stream.tile([P, PACK, w], U8, name="b_raw", bufs=5)
+            nc.sync.dma_start(out=t[:], in_=wb_bytes[g * 512:(g + 1) * 512, n0:n0 + w].rearrange("(p j) n -> p j n", j=PACK))
+            st[i]["b_raw"] = t
+
+        def widen(i):
+            if not 0 <= i < n:
+                return
+            ci, g, n0, w = steps[i]
+            t = stream.tile([P, PACK, w], BF16, name="b_wide", bufs=3)
+            for j in range(PACK):
+                nc.scalar.activation(out=t[:, j, :], in_=st[i]["b_raw"][:, j, :].bitcast(F8), func=ACT.Copy, scale=wbs[:, 4 * g + j:4 * g + j + 1])
+            st[i]["b_wide"] = t
+
+        def interleave(copy, dst, src, c0, c1):
+            copy(out=dst[:, c0:c1, :].rearrange("p (c i) t -> p c t i", i=4), in_=src[:, :, c0:c1].rearrange("p t (c i) -> p c t i", i=4))
+
+        def split(i):
+            ci, g, n0, w = steps[i]
+            return w - (w * S_SHARE // 16)
+
+        def s_inter(i):
+            if not 0 <= i < n:
+                return
+            ci, g, n0, w = steps[i]
+            t = stream.tile([P, w, PACK], BF16, name="w_il", bufs=3, align_bytes=64)
+            st[i]["w_il"] = t
+            if split(i) < w:
+                interleave(nc.scalar.copy, t, st[i]["w_raw"], split(i), w)
+
+        def v_inter_w(i):
+            if not 0 <= i < n:
+                return
+            interleave(nc.vector.tensor_copy, st[i]["w_il"], st[i]["w_raw"], 0, split(i))
+
+        def v_inter_b(i):
+            if not 0 <= i < n:
+                return
+            ci, g, n0, w = steps[i]
+            t = stream.tile([P, w, PACK], BF16, name="b_il", bufs=2, align_bytes=64)
+            st[i]["b_il"] = t
+            interleave(nc.vector.tensor_copy, t, st[i]["b_wide"], 0, w)
+
+        def quant(i, il, name, bufs):
+            ci, g, n0, w = steps[i]
+            q = stream.tile([P, w], U32, name=name + "_q", bufs=bufs, align_bytes=64)
+            z = stream.tile([P, w], U8, name=name + "_z", bufs=bufs, align_bytes=64)
+            nc.vector.quantize_mx(out=q[:].bitcast(X4), scales=z[:], in_=il[:].rearrange("p w t -> p (w t)"))
+            return q, z
+
+        def quant_w(i):
+            st[i]["w_q"] = quant(i, st[i]["w_il"], "w", 3)
+
+        def quant_b(i):
+            st[i]["b_q"] = quant(i, st[i]["b_il"], "b", 7)
+
+        def mm(i, key, left, times):
+            ci, g, n0, w = steps[i]
+            q, z = st[i][key]
+            lq, lz = left
+            bw = min(w, BANK)
+            for h in range(w // bw):
+                k = (ci, h)
+                if k not in acc:
+                    acc[k] = psum.tile([P, bw], F32, name="acc", bufs=4)
+                    count[k] = 0
+                for r in range(times):
+                    count[k] += 1
+                    nc.tensor.matmul_mx(
+                        out=acc[k][:],
+                        lhsT=lq[:, g * P:(g + 1) * P].bitcast(X4),
+                        lhsT_scale=lz[:, g * P:(g + 1) * P],
+                        rhs=q[:, h * bw:(h + 1) * bw].bitcast(X4),
+                        rhs_scale=z[:, h * bw:(h + 1) * bw],
+                        start=(count[k] == 1),
+                        stop=(count[k] == 20),
+                    )
+
+        waiting = {"w_q": [], "b_q": []}
+        left = {}
+
+        def multiply(i, key):
+            waiting[key].append(i)
+            if key in left:
+                for k in waiting[key]:
+                    mm(k, key, left[key], 2 if key == "w_q" else 3)
+                waiting[key].clear()
+
+        def arrived(key, codes):
+            left[key] = codes
+            for k in waiting[key]:
+                mm(k, key, left[key], 2 if key == "w_q" else 3)
+            waiting[key].clear()
+
+        def leave(ci):
+            n0 = sum(CHUNKS[:ci])
+            bw = min(CHUNKS[ci], BANK)
+            for h in range(CHUNKS[ci] // bw):
+                o = stream.tile([P, bw], F32, name="o", bufs=3)
+                nc.scalar.activation(out=o[:], in_=acc[(ci, h)][:], func=ACT.Copy, scale=0.5)
+                nc.sync.dma_start(out=out[:, n0 + h * bw:n0 + (h + 1) * bw], in_=o[:])
+
+        one = keep.tile([P, 1], F32)
+        nc.vector.memset(one[:], 1.0)
+        warm = keep.tile([P, 1], F32)
+        nc.scalar.activation(out=warm[:], in_=one[:], func=ACT.Exp)
+        load_b(0)
+        wbs = keep.tile([P, 16], F32)
+        nc.sync.dma_start(out=wbs[:].rearrange("p (g t) -> p g t", t=4), in_=wb_scale.rearrange("(g p t) o -> p g (t o)", p=P, t=4))
+        ident = keep.tile([P, P], F32)
+        make_identity(nc, ident[:])
+        ident16 = keep.tile([P, P], BF16)
+        nc.gpsimd.tensor_copy(out=ident16[:], in_=ident[:])
+        c_sb = keep.tile([P, P], BF16)
+        nc.gpsimd.memset(c_sb[:], 0.0)
+        neg_half = keep.tile([P, P], F32)
+        nc.gpsimd.memset(neg_half[:], -0.5)
+        load_w(0)
+        x_sb = keep.tile([P, D], BF16)
+        nc.sync.dma_start(out=x_sb[:], in_=x)
+        load_b(1)
+        load_w(1)
+        wa_sb = keep.tile([P, G, PACK, R], BF16)
+        nc.sync.dma_start(out=wa_sb[:], in_=wa.rearrange("(g p j) r -> p g j r", p=P, j=PACK))
+        load_b(2)
+        load_w(2)
+        load_b(3)
+        load_w(3)
+        nc.sync.dma_start(out=c_sb[0:E, :], in_=c)
+        load_b(4)
+        load_w(4)
+        s_bc = keep.tile([P, E * R], BF16)
+        nc.sync.dma_start(out=s_bc[:], in_=s.partition_broadcast(P))
+
+        def words_to_codes(src, name):
+            words = src[:].bitcast(F32)
+            grouped = keep.tile([P, G, P, PACK], BF16, name=name + "_g", align_bytes=64)
+            for half in range(2):
+                bank = psum.tile([P, 2, 2, P], F32, name="turned", bufs=2)
+                for gg in range(2):
+                    g = 2 * half + gg
+                    for u in range(2):
+                        nc.tensor.transpose(bank[:, gg, u, :], words[:, 256 * g + u:256 * (g + 1):2], ident[:])
+                view = grouped[:, 2 * half:2 * half + 2, :, :].rearrange("p g r t -> p g (r t)").bitcast(F32).rearrange("p g (r u) -> p g r u", u=2)
+                nc.vector.tensor_copy(out=view, in_=bank[:].rearrange("p g u r -> p g r u"))
+            return grouped
+
+        def quant_keep(grouped, name):
+            q = keep.tile([P, 512], U32, name=name + "_q", align_bytes=64)
+            z = keep.tile([P, 512], U8, name=name + "_z", align_bytes=64)
+            nc.vector.quantize_mx(out=q[:].bitcast(X4), scales=z[:], in_=grouped[:].rearrange("p g r t -> p (g r t)"))
+            return q, z
+
+        v = {}
+
+        def e_x():
+            v["x_g"] = words_to_codes(x_sb, "x")
+
+        def e_wa():
+            v["wa_g"] = keep.tile([P, G, R, PACK], BF16, name="wa_g", align_bytes=64)
+            nc.vector.tensor_copy(out=v["wa_g"][:], in_=wa_sb[:].rearrange("p g j r -> p g r j"))
+            v["x"] = quant_keep(v["x_g"], "x")
+            arrived("w_q", v["x"])
+
+        def e_a():
+            v["wa"] = quant_keep(v["wa_g"], "wa")
+            a_ps = psum.tile([P, 2, P], F32, name="a_ps")
+            v["a"] = a_ps
+            xq, xz = v["x"]
+            aq, az = v["wa"]
+            for side in range(2):
+                for g in range(G):
+                    cols = slice(g * P, (g + 1) * P)
+                    l, r = (v["wa"], v["x"]) if side == 0 else (v["x"], v["wa"])
+                    nc.tensor.matmul_mx(out=a_ps[:, side, :], lhsT=l[0][:, cols].bitcast(X4), lhsT_scale=l[1][:, cols],
+                                        rhs=r[0][:, cols].bitcast(X4), rhs_scale=r[1][:, cols], start=(g == 0), stop=(g == G - 1))
+            ct_ps = psum.tile([P, P], BF16, name="small")
+            nc.tensor.transpose(ct_ps[:], c_sb[:], ident16[:])
+            v["aT"] = keep.tile([P, P], F32, name="aT")
+            nc.scalar.copy(out=v["aT"][:], in_=a_ps[:, 0, :])
+            v["cT"] = keep.tile([P, E], F32, name="cT")
+            nc.scalar.copy(out=v["cT"][:], in_=ct_ps[:, 0:E])
+
+        def e_logits():
+            cT = v["cT"]
+            cT2 = keep.tile([P, E], F32)
+            nc.vector.tensor_tensor(out=cT2[:], in0=cT[:], in1=cT[:], op=ALU.mult)
+            lg = psum.tile([P, E], F32, name="small")
+            nc.tensor.matmul(lg[:], lhsT=v["aT"][:], rhs=cT[:], start=True, stop=False)
+            nc.tensor.matmul(lg[:], lhsT=neg_half[:], rhs=cT2[:], start=False, stop=True)
+            v["lg"] = lg
+
+        def e_exp():
+            lg = v["lg"]
+            top = keep.tile([P, 1], F32)
+            nc.vector.reduce_max(out=top[:], in_=lg[:], axis=AX.X)
+            ntop = keep.tile([P, 1], F32)
+            nc.vector.tensor_scalar(out=ntop[:], in0=top[:], scalar1=-0.125, scalar2=None, op0=ALU.mult)
+            v["ex"] = keep.tile([P, E], F32, name="ex")
+            v["total"] = keep.tile([P, 1], F32, name="total")
+            nc.scalar.activation(out=v["ex"][:], in_=lg[:], func=ACT.Exp, bias=ntop[:], scale=0.125, accum_out=v["total"][:])
+
+        def e_zs():
+            inv = keep.tile([P, 1], F32)
+            nc.vector.reciprocal(out=inv[:], in_=v["total"][:])
+            gate = keep.tile([P, E], F32)
+            nc.vector.tensor_scalar(out=gate[:], in0=v["ex"][:], scalar1=inv[:], scalar2=None, op0=ALU.mult)
+            zs = keep.tile([P, E * R], BF16)
+            for e in range(E):
+                cols = slice(e * R, (e + 1) * R)
+                nc.vector.scalar_tensor_tensor(out=zs[:, cols], in0=v["a"][:, 1, :], scalar=gate[:, e:e + 1], in1=s_bc[:, cols], op0=ALU.mult, op1=ALU.mult)
+            v["zs"] = zs
+
+        def e_turn():
+            v["zs_g"] = words_to_codes(v["zs"], "zs")
+
+        def e_codes():
+            arrived("b_q", quant_keep(v["zs_g"], "zs"))
+
+        full = []
+        done = []
+        extra = {0: [e_x], 1: [e_wa], 2: [e_a], 3: [e_logits], 4: [e_exp, e_zs], 5: [e_turn], 6: [e_codes]}
+
+        widen(0)
+        s_inter(0)
+        v_inter_w(0)
+        widen(1)
+        v_inter_b(0)
+        for i in range(n):
+            s_inter(i + 1)
+            widen(i + 2)
+            quant_w(i)
+            multiply(i, "w_q")
+            v_inter_w(i + 1)
+            quant_b(i)
+            multiply(i, "b_q")
+            v_inter_b(i + 1)
+            for f in extra.get(i, []):
+                f()
+            load_b(i + 5)
+            load_w(i + 5)
+            for ci in sorted(full):
+                leave(ci)
+                full.remove(ci)
+            for ci in range(len(CHUNKS)):
+                if ci not in done and (ci, 0) in count and all(count[k] == 20 for k in count if k[0] == ci):
+                    full.append(ci)
+                    done.append(ci)
+        for ci in full:
+            leave(ci)

@@ -21,7 +21,8 @@ PACK = 4
 G = 4
 BANK = 512
 CHUNKS = [256,512,1024,1024,1024,256]
-S_SHARE = 6
+S_SHARE = 12
+TENSOR_COLS = 256
 
 
 def tile_hydraloraprototyperouted_w_kernel(tc, x, w0, wa, c, s, wb_bytes, wb_scale, out):
@@ -73,7 +74,20 @@ def tile_hydraloraprototyperouted_w_kernel(tc, x, w0, wa, c, s, wb_bytes, wb_sca
 
         def split(i):
             ci, g, n0, w = steps[i]
-            return w - (w * S_SHARE // 16)
+            return w - (w * (15 if w == 1024 else S_SHARE) // 32)
+
+        def by_tensor(i):
+            return TENSOR_COLS if (0 <= i < n and steps[i][3] == 1024) else 0
+
+        def t_inter(i):
+            if by_tensor(i) == 0:
+                return
+            w = steps[i][3]
+            bank = psum.tile([P, 2, 2 * P * PACK // 2], BF16, name="turned", bufs=2)
+            for h in range(2):
+                c0 = w - TENSOR_COLS + h * P
+                nc.tensor.matmul(bank[:, h, :], lhsT=ident16[:], rhs=st[i]["w_raw"][:, :, c0:c0 + P].rearrange("p j n -> p n j"), start=True, stop=True)
+            st[i]["bank"] = bank
 
         def s_inter(i):
             if not 0 <= i < n:
@@ -81,8 +95,11 @@ def tile_hydraloraprototyperouted_w_kernel(tc, x, w0, wa, c, s, wb_bytes, wb_sca
             ci, g, n0, w = steps[i]
             t = stream.tile([P, w, PACK], BF16, name="w_il", bufs=3, align_bytes=64)
             st[i]["w_il"] = t
-            if split(i) < w:
-                interleave(nc.scalar.copy, t, st[i]["w_raw"], split(i), w)
+            end = w - by_tensor(i)
+            if end < w:
+                nc.scalar.copy(out=t[:, end:w, :].rearrange("p w t -> p (w t)"), in_=st[i]["bank"][:].rearrange("p h c -> p (h c)"))
+            if split(i) < end:
+                interleave(nc.scalar.copy, t, st[i]["w_raw"], split(i), end)
 
         def v_inter_w(i):
             if not 0 <= i < n:
@@ -198,7 +215,7 @@ def tile_hydraloraprototyperouted_w_kernel(tc, x, w0, wa, c, s, wb_bytes, wb_sca
                     for u in range(2):
                         nc.tensor.transpose(bank[:, gg, u, :], words[:, 256 * g + u:256 * (g + 1):2], ident[:])
                 view = grouped[:, 2 * half:2 * half + 2, :, :].rearrange("p g r t -> p g (r t)").bitcast(F32).rearrange("p g (r u) -> p g r u", u=2)
-                nc.vector.tensor_copy(out=view, in_=bank[:].rearrange("p g u r -> p g r u"))
+                nc.scalar.copy(out=view, in_=bank[:].rearrange("p g u r -> p g r u"))
             return grouped
 
         def quant_keep(grouped, name):
@@ -283,6 +300,7 @@ def tile_hydraloraprototyperouted_w_kernel(tc, x, w0, wa, c, s, wb_bytes, wb_sca
         widen(1)
         v_inter_b(0)
         for i in range(n):
+            t_inter(i + 2)
             s_inter(i + 1)
             widen(i + 2)
             quant_w(i)

@@ -21,7 +21,7 @@ PACK = 4
 G = 4
 BANK = 512
 CHUNKS = [256,512,1024,1024,1024,256]
-S_SHARE = 12
+S_SHARE = 8
 TENSOR_COLS = 256
 
 
@@ -74,7 +74,7 @@ def tile_hydraloraprototyperouted_w_kernel(tc, x, w0, wa, c, s, wb_bytes, wb_sca
 
         def split(i):
             ci, g, n0, w = steps[i]
-            return w - (w * (15 if w == 1024 else S_SHARE) // 32)
+            return w - (w * (8 if w == 1024 else S_SHARE) // 32)
 
         def by_tensor(i):
             return TENSOR_COLS if (0 <= i < n and steps[i][3] == 1024) else 0

@@ -20,9 +20,12 @@ P = 128
 PACK = 4
 G = 4
 BANK = 512
-CHUNKS = [256,512,1024,1024,1024,256]
-S_SHARE = 8
-TENSOR_COLS = 256
+BASE_TIMES = 2
+LOW_TIMES = 3
+DELAY = 2
+STEPS = [(0, 256, [0]), (0, 256, [1]), (0, 256, [2,3]), (256, 512, [0,1]), (256, 512, [2,3]), (768, 1024, [0]), (768, 1024, [1]), (768, 1024, [2]), (768, 1024, [3]), (1792, 1024, [0]), (1792, 1024, [1]), (1792, 1024, [2]), (1792, 1024, [3]), (2816, 1024, [0]), (2816, 1024, [1]), (2816, 1024, [2]), (2816, 1024, [3]), (3840, 128, [0,1,2,3]), (3968, 128, [0,1,2,3])]
+SCALAR_COLS = [0, 0, 0, 0, 0, 0, 208, 208, 208, 208, 208, 208, 208, 208, 208, 208, 464, 224, 224]
+TENSOR_COLS = [0, 0, 0, 0, 256, 256, 256, 256, 256, 256, 256, 256, 256, 256, 256, 256, 0, 0, 0]
 
 
 def tile_hydraloraprototyperouted_w_kernel(tc, x, w0, wa, c, s, wb_bytes, wb_scale, out):
@@ -33,121 +36,116 @@ def tile_hydraloraprototyperouted_w_kernel(tc, x, w0, wa, c, s, wb_bytes, wb_sca
         psum = ctx.enter_context(tc.psum_pool(name="psum", bufs=1))
         ctx.enter_context(tc.manual_schedule())
 
-        steps = []
-        n0 = 0
-        for ci, w in enumerate(CHUNKS):
-            for g in range(G):
-                steps.append((ci, g, n0, w))
-            n0 += w
-        n = len(steps)
+        n = len(STEPS)
         st = [dict() for i in range(n)]
         acc = {}
         count = {}
 
+        def cols(i):
+            n0, w, gs = STEPS[i]
+            return w * len(gs)
+
+        def size(i):
+            return "wide" if cols(i) > 256 else "narrow"
+
         def load_w(i):
-            if not 0 <= i < n:
+            if i >= n:
                 return
-            ci, g, n0, w = steps[i]
-            t = stream.tile([P, PACK, w], BF16, name="w_raw", bufs=5)
-            nc.sync.dma_start(out=t[:], in_=w0[g * 512:(g + 1) * 512, n0:n0 + w].rearrange("(p j) n -> p j n", j=PACK))
-            st[i]["w_raw"] = t
+            n0, w, gs = STEPS[i]
+            W = cols(i)
+            t = stream.tile([P, PACK, 2 * W], BF16, name="raw_" + size(i), bufs=4)
+            for k, g in enumerate(gs):
+                nc.sync.dma_start(out=t[:, :, W + k * w:W + (k + 1) * w], in_=w0[g * 512:(g + 1) * 512, n0:n0 + w].rearrange("(p j) n -> p j n", j=PACK))
+            st[i]["raw"] = t
 
         def load_b(i):
-            if not 0 <= i < n:
+            if i >= n:
                 return
-            ci, g, n0, w = steps[i]
-            t = stream.tile([P, PACK, w], U8, name="b_raw", bufs=5)
-            nc.sync.dma_start(out=t[:], in_=wb_bytes[g * 512:(g + 1) * 512, n0:n0 + w].rearrange("(p j) n -> p j n", j=PACK))
+            n0, w, gs = STEPS[i]
+            t = stream.tile([P, PACK, cols(i)], U8, name="b_raw_" + size(i), bufs=4)
+            for k, g in enumerate(gs):
+                nc.sync.dma_start(out=t[:, :, k * w:(k + 1) * w], in_=wb_bytes[g * 512:(g + 1) * 512, n0:n0 + w].rearrange("(p j) n -> p j n", j=PACK))
             st[i]["b_raw"] = t
 
         def widen(i):
-            if not 0 <= i < n:
+            if i >= n:
                 return
-            ci, g, n0, w = steps[i]
-            t = stream.tile([P, PACK, w], BF16, name="b_wide", bufs=3)
-            for j in range(PACK):
-                nc.scalar.activation(out=t[:, j, :], in_=st[i]["b_raw"][:, j, :].bitcast(F8), func=ACT.Copy, scale=wbs[:, 4 * g + j:4 * g + j + 1])
-            st[i]["b_wide"] = t
+            n0, w, gs = STEPS[i]
+            t = st[i]["raw"]
+            for k, g in enumerate(gs):
+                for j in range(PACK):
+                    nc.scalar.activation(out=t[:, j, k * w:(k + 1) * w], in_=st[i]["b_raw"][:, j, k * w:(k + 1) * w].bitcast(F8), func=ACT.Copy, scale=wbs[:, 4 * g + j:4 * g + j + 1])
 
         def interleave(copy, dst, src, c0, c1):
             copy(out=dst[:, c0:c1, :].rearrange("p (c i) t -> p c t i", i=4), in_=src[:, :, c0:c1].rearrange("p t (c i) -> p c t i", i=4))
 
-        def split(i):
-            ci, g, n0, w = steps[i]
-            return w - (w * (8 if w == 1024 else S_SHARE) // 32)
-
-        def by_tensor(i):
-            return TENSOR_COLS if (0 <= i < n and steps[i][3] == 1024) else 0
-
         def t_inter(i):
-            if by_tensor(i) == 0:
+            if i >= n or TENSOR_COLS[i] == 0:
                 return
-            w = steps[i][3]
-            bank = psum.tile([P, 2, 2 * P * PACK // 2], BF16, name="turned", bufs=2)
-            for h in range(2):
-                c0 = w - TENSOR_COLS + h * P
-                nc.tensor.matmul(bank[:, h, :], lhsT=ident16[:], rhs=st[i]["w_raw"][:, :, c0:c0 + P].rearrange("p j n -> p n j"), start=True, stop=True)
+            W = cols(i)
+            bank = psum.tile([P, TENSOR_COLS[i], PACK], BF16, name="turned", bufs=2)
+            for h in range(TENSOR_COLS[i] // P):
+                c0 = 2 * W - TENSOR_COLS[i] + h * P
+                nc.tensor.matmul(bank[:, h * P:(h + 1) * P, :].rearrange("p n j -> p (n j)"), lhsT=ident16[:], rhs=st[i]["raw"][:, :, c0:c0 + P].rearrange("p j n -> p n j"), start=True, stop=True)
             st[i]["bank"] = bank
 
         def s_inter(i):
-            if not 0 <= i < n:
+            if i >= n:
                 return
-            ci, g, n0, w = steps[i]
-            t = stream.tile([P, w, PACK], BF16, name="w_il", bufs=3, align_bytes=64)
-            st[i]["w_il"] = t
-            end = w - by_tensor(i)
-            if end < w:
-                nc.scalar.copy(out=t[:, end:w, :].rearrange("p w t -> p (w t)"), in_=st[i]["bank"][:].rearrange("p h c -> p (h c)"))
-            if split(i) < end:
-                interleave(nc.scalar.copy, t, st[i]["w_raw"], split(i), end)
+            W = cols(i)
+            t = stream.tile([P, 2 * W, PACK], BF16, name="il_" + size(i), bufs=2, align_bytes=64)
+            st[i]["il"] = t
+            end = 2 * W - TENSOR_COLS[i]
+            if end < 2 * W:
+                nc.scalar.copy(out=t[:, end:2 * W, :].rearrange("p w t -> p (w t)"), in_=st[i]["bank"][:].rearrange("p n j -> p (n j)"))
+            if SCALAR_COLS[i] > 0:
+                interleave(nc.scalar.copy, t, st[i]["raw"], end - SCALAR_COLS[i], end)
 
-        def v_inter_w(i):
-            if not 0 <= i < n:
+        def v_inter(i, c0=0, c1=None):
+            if i >= n:
                 return
-            interleave(nc.vector.tensor_copy, st[i]["w_il"], st[i]["w_raw"], 0, split(i))
+            W = cols(i)
+            interleave(nc.vector.tensor_copy, st[i]["il"], st[i]["raw"], c0, 2 * W - TENSOR_COLS[i] - SCALAR_COLS[i] if c1 is None else c1)
 
-        def v_inter_b(i):
-            if not 0 <= i < n:
-                return
-            ci, g, n0, w = steps[i]
-            t = stream.tile([P, w, PACK], BF16, name="b_il", bufs=2, align_bytes=64)
-            st[i]["b_il"] = t
-            interleave(nc.vector.tensor_copy, t, st[i]["b_wide"], 0, w)
+        def v_inter_first():
+            v_inter(0, c0=cols(0))
+            v_inter(0, c1=cols(0))
 
         def quant(i, il, name, bufs):
-            ci, g, n0, w = steps[i]
-            q = stream.tile([P, w], U32, name=name + "_q", bufs=bufs, align_bytes=64)
-            z = stream.tile([P, w], U8, name=name + "_z", bufs=bufs, align_bytes=64)
-            nc.vector.quantize_mx(out=q[:].bitcast(X4), scales=z[:], in_=il[:].rearrange("p w t -> p (w t)"))
+            q = stream.tile([P, cols(i)], U32, name=name + "_q_" + size(i), bufs=bufs, align_bytes=64)
+            z = stream.tile([P, cols(i)], U8, name=name + "_z_" + size(i), bufs=bufs, align_bytes=64)
+            nc.vector.quantize_mx(out=q[:].bitcast(X4), scales=z[:], in_=il.rearrange("p w t -> p (w t)"))
             return q, z
 
         def quant_w(i):
-            st[i]["w_q"] = quant(i, st[i]["w_il"], "w", 3)
+            st[i]["w_q"] = quant(i, st[i]["il"][:, cols(i):2 * cols(i), :], "w", 2)
 
         def quant_b(i):
-            st[i]["b_q"] = quant(i, st[i]["b_il"], "b", 7)
+            st[i]["b_q"] = quant(i, st[i]["il"][:, 0:cols(i), :], "b", 4)
 
-        def mm(i, key, left, times):
-            ci, g, n0, w = steps[i]
+        def mm(i, key):
+            times = BASE_TIMES if key == "w_q" else LOW_TIMES
+            n0, w, gs = STEPS[i]
             q, z = st[i][key]
-            lq, lz = left
+            lq, lz = left[key]
             bw = min(w, BANK)
-            for h in range(w // bw):
-                k = (ci, h)
-                if k not in acc:
-                    acc[k] = psum.tile([P, bw], F32, name="acc", bufs=4)
-                    count[k] = 0
-                for r in range(times):
-                    count[k] += 1
-                    nc.tensor.matmul_mx(
-                        out=acc[k][:],
-                        lhsT=lq[:, g * P:(g + 1) * P].bitcast(X4),
-                        lhsT_scale=lz[:, g * P:(g + 1) * P],
-                        rhs=q[:, h * bw:(h + 1) * bw].bitcast(X4),
-                        rhs_scale=z[:, h * bw:(h + 1) * bw],
-                        start=(count[k] == 1),
-                        stop=(count[k] == 20),
-                    )
+            for k, g in enumerate(gs):
+                for h in range(w // bw):
+                    b = n0 + h * bw
+                    if b not in acc:
+                        acc[b] = psum.tile([P, bw], F32, name="acc", bufs=4)
+                        count[b] = 0
+                    for r in range(times):
+                        count[b] += 1
+                        nc.tensor.matmul_mx(
+                            out=acc[b][:],
+                            lhsT=lq[:, g * P:(g + 1) * P].bitcast(X4),
+                            lhsT_scale=lz[:, g * P:(g + 1) * P],
+                            rhs=q[:, k * w + h * bw:k * w + (h + 1) * bw].bitcast(X4),
+                            rhs_scale=z[:, k * w + h * bw:k * w + (h + 1) * bw],
+                            start=(count[b] == 1),
+                            stop=(count[b] == G * (BASE_TIMES + LOW_TIMES)),
+                        )
 
         waiting = {"w_q": [], "b_q": []}
         left = {}
@@ -156,30 +154,25 @@ def tile_hydraloraprototyperouted_w_kernel(tc, x, w0, wa, c, s, wb_bytes, wb_sca
             waiting[key].append(i)
             if key in left:
                 for k in waiting[key]:
-                    mm(k, key, left[key], 2 if key == "w_q" else 3)
+                    mm(k, key)
                 waiting[key].clear()
 
         def arrived(key, codes):
             left[key] = codes
             for k in waiting[key]:
-                mm(k, key, left[key], 2 if key == "w_q" else 3)
+                mm(k, key)
             waiting[key].clear()
 
-        def leave(ci):
-            n0 = sum(CHUNKS[:ci])
-            bw = min(CHUNKS[ci], BANK)
-            for h in range(CHUNKS[ci] // bw):
-                o = stream.tile([P, bw], F32, name="o", bufs=3)
-                nc.scalar.activation(out=o[:], in_=acc[(ci, h)][:], func=ACT.Copy, scale=0.5)
-                nc.sync.dma_start(out=out[:, n0 + h * bw:n0 + (h + 1) * bw], in_=o[:])
+        def leave(b):
+            bw = acc[b].shape[1]
+            o = stream.tile([P, bw], F32, name="o", bufs=3)
+            nc.scalar.activation(out=o[:], in_=acc[b][:], func=ACT.Copy, scale=0.5)
+            nc.sync.dma_start(out=out[:, b:b + bw], in_=o[:])
 
         one = keep.tile([P, 1], F32)
         nc.vector.memset(one[:], 1.0)
         warm = keep.tile([P, 1], F32)
         nc.scalar.activation(out=warm[:], in_=one[:], func=ACT.Exp)
-        load_b(0)
-        wbs = keep.tile([P, 16], F32)
-        nc.sync.dma_start(out=wbs[:].rearrange("p (g t) -> p g t", t=4), in_=wb_scale.rearrange("(g p t) o -> p g (t o)", p=P, t=4))
         ident = keep.tile([P, P], F32)
         make_identity(nc, ident[:])
         ident16 = keep.tile([P, P], BF16)
@@ -188,34 +181,63 @@ def tile_hydraloraprototyperouted_w_kernel(tc, x, w0, wa, c, s, wb_bytes, wb_sca
         nc.gpsimd.memset(c_sb[:], 0.0)
         neg_half = keep.tile([P, P], F32)
         nc.gpsimd.memset(neg_half[:], -0.5)
+        x_sb = keep.tile([P, D], BF16, name="rows")
+        wa_sb = keep.tile([P, G, PACK, R], BF16)
+        s_bc = keep.tile([P, E * R], BF16)
+        wbs = keep.tile([P, 16], F32)
+
+        def load_wbs():
+            nc.sync.dma_start(out=wbs[:].rearrange("p (g t) -> p g t", t=4), in_=wb_scale.rearrange("(g p t) o -> p g (t o)", p=P, t=4))
+
+        def load_x():
+            nc.sync.dma_start(out=x_sb[:], in_=x)
+
+        def load_wa():
+            nc.sync.dma_start(out=wa_sb[:], in_=wa.rearrange("(g p j) r -> p g j r", p=P, j=PACK))
+
+        def load_c():
+            nc.sync.dma_start(out=c_sb[0:E, :], in_=c)
+
+        def load_s():
+            nc.sync.dma_start(out=s_bc[:], in_=s.partition_broadcast(P))
+
+        load_wbs()
+        load_b(0)
         load_w(0)
-        x_sb = keep.tile([P, D], BF16)
-        nc.sync.dma_start(out=x_sb[:], in_=x)
         load_b(1)
         load_w(1)
-        wa_sb = keep.tile([P, G, PACK, R], BF16)
-        nc.sync.dma_start(out=wa_sb[:], in_=wa.rearrange("(g p j) r -> p g j r", p=P, j=PACK))
         load_b(2)
         load_w(2)
+        load_x()
+        load_wa()
         load_b(3)
         load_w(3)
-        nc.sync.dma_start(out=c_sb[0:E, :], in_=c)
+        load_c()
         load_b(4)
         load_w(4)
-        s_bc = keep.tile([P, E * R], BF16)
-        nc.sync.dma_start(out=s_bc[:], in_=s.partition_broadcast(P))
+        load_s()
+        load_b(5)
+        load_w(5)
+        load_b(6)
+        load_w(6)
 
-        def words_to_codes(src, name):
+        def turn(src, name):
             words = src[:].bitcast(F32)
-            grouped = keep.tile([P, G, P, PACK], BF16, name=name + "_g", align_bytes=64)
+            banks = []
             for half in range(2):
                 bank = psum.tile([P, 2, 2, P], F32, name="turned", bufs=2)
                 for gg in range(2):
                     g = 2 * half + gg
                     for u in range(2):
                         nc.tensor.transpose(bank[:, gg, u, :], words[:, 256 * g + u:256 * (g + 1):2], ident[:])
+                banks.append(bank)
+            return banks
+
+        def group(banks, name, copy):
+            grouped = keep.tile([P, G, P, PACK], BF16, name="rows_g", align_bytes=64)
+            for half in range(2):
                 view = grouped[:, 2 * half:2 * half + 2, :, :].rearrange("p g r t -> p g (r t)").bitcast(F32).rearrange("p g (r u) -> p g r u", u=2)
-                nc.scalar.copy(out=view, in_=bank[:].rearrange("p g u r -> p g r u"))
+                copy(out=view, in_=banks[half][:].rearrange("p g u r -> p g r u"))
             return grouped
 
         def quant_keep(grouped, name):
@@ -226,35 +248,41 @@ def tile_hydraloraprototyperouted_w_kernel(tc, x, w0, wa, c, s, wb_bytes, wb_sca
 
         v = {}
 
-        def e_x():
-            v["x_g"] = words_to_codes(x_sb, "x")
+        def turn_x():
+            v["x_b"] = turn(x_sb, "x")
 
-        def e_wa():
+        def group_x():
+            v["x_g"] = group(v["x_b"], "x", nc.scalar.copy)
+
+        def inter_wa():
             v["wa_g"] = keep.tile([P, G, R, PACK], BF16, name="wa_g", align_bytes=64)
             nc.vector.tensor_copy(out=v["wa_g"][:], in_=wa_sb[:].rearrange("p g j r -> p g r j"))
+
+        def quant_x():
             v["x"] = quant_keep(v["x_g"], "x")
             arrived("w_q", v["x"])
 
-        def e_a():
+        def mm_a():
             v["wa"] = quant_keep(v["wa_g"], "wa")
             a_ps = psum.tile([P, 2, P], F32, name="a_ps")
             v["a"] = a_ps
-            xq, xz = v["x"]
-            aq, az = v["wa"]
             for side in range(2):
                 for g in range(G):
-                    cols = slice(g * P, (g + 1) * P)
+                    cc = slice(g * P, (g + 1) * P)
                     l, r = (v["wa"], v["x"]) if side == 0 else (v["x"], v["wa"])
-                    nc.tensor.matmul_mx(out=a_ps[:, side, :], lhsT=l[0][:, cols].bitcast(X4), lhsT_scale=l[1][:, cols],
-                                        rhs=r[0][:, cols].bitcast(X4), rhs_scale=r[1][:, cols], start=(g == 0), stop=(g == G - 1))
+                    nc.tensor.matmul_mx(out=a_ps[:, side, :], lhsT=l[0][:, cc].bitcast(X4), lhsT_scale=l[1][:, cc],
+                                        rhs=r[0][:, cc].bitcast(X4), rhs_scale=r[1][:, cc], start=(g == 0), stop=(g == G - 1))
             ct_ps = psum.tile([P, P], BF16, name="small")
             nc.tensor.transpose(ct_ps[:], c_sb[:], ident16[:])
-            v["aT"] = keep.tile([P, P], F32, name="aT")
-            nc.scalar.copy(out=v["aT"][:], in_=a_ps[:, 0, :])
-            v["cT"] = keep.tile([P, E], F32, name="cT")
-            nc.scalar.copy(out=v["cT"][:], in_=ct_ps[:, 0:E])
+            v["ct_ps"] = ct_ps
 
-        def e_logits():
+        def copy_a():
+            v["aT"] = keep.tile([P, P], F32, name="aT")
+            nc.scalar.copy(out=v["aT"][:], in_=v["a"][:, 0, :])
+            v["cT"] = keep.tile([P, E], F32, name="cT")
+            nc.scalar.copy(out=v["cT"][:], in_=v["ct_ps"][:, 0:E])
+
+        def logits():
             cT = v["cT"]
             cT2 = keep.tile([P, E], F32)
             nc.vector.tensor_tensor(out=cT2[:], in0=cT[:], in1=cT[:], op=ALU.mult)
@@ -263,7 +291,7 @@ def tile_hydraloraprototyperouted_w_kernel(tc, x, w0, wa, c, s, wb_bytes, wb_sca
             nc.tensor.matmul(lg[:], lhsT=neg_half[:], rhs=cT2[:], start=False, stop=True)
             v["lg"] = lg
 
-        def e_exp():
+        def expo():
             lg = v["lg"]
             top = keep.tile([P, 1], F32)
             nc.vector.reduce_max(out=top[:], in_=lg[:], axis=AX.X)
@@ -273,52 +301,58 @@ def tile_hydraloraprototyperouted_w_kernel(tc, x, w0, wa, c, s, wb_bytes, wb_sca
             v["total"] = keep.tile([P, 1], F32, name="total")
             nc.scalar.activation(out=v["ex"][:], in_=lg[:], func=ACT.Exp, bias=ntop[:], scale=0.125, accum_out=v["total"][:])
 
-        def e_zs():
+        def make_zs():
             inv = keep.tile([P, 1], F32)
             nc.vector.reciprocal(out=inv[:], in_=v["total"][:])
             gate = keep.tile([P, E], F32)
             nc.vector.tensor_scalar(out=gate[:], in0=v["ex"][:], scalar1=inv[:], scalar2=None, op0=ALU.mult)
-            zs = keep.tile([P, E * R], BF16)
+            zs = keep.tile([P, E * R], BF16, name="rows")
             for e in range(E):
-                cols = slice(e * R, (e + 1) * R)
-                nc.vector.scalar_tensor_tensor(out=zs[:, cols], in0=v["a"][:, 1, :], scalar=gate[:, e:e + 1], in1=s_bc[:, cols], op0=ALU.mult, op1=ALU.mult)
+                cc = slice(e * R, (e + 1) * R)
+                nc.vector.scalar_tensor_tensor(out=zs[:, cc], in0=v["a"][:, 1, :], scalar=gate[:, e:e + 1], in1=s_bc[:, cc], op0=ALU.mult, op1=ALU.mult)
             v["zs"] = zs
+            v["z_b"] = turn(zs, "zs")
 
-        def e_turn():
-            v["zs_g"] = words_to_codes(v["zs"], "zs")
+        def group_zs():
+            v["zs_g"] = group(v["z_b"], "zs", nc.scalar.copy)
 
-        def e_codes():
+        def quant_zs():
             arrived("b_q", quant_keep(v["zs_g"], "zs"))
 
-        full = []
+        after = {2: [turn_x, group_x], 5: [inter_wa, quant_x], 6: [mm_a, copy_a], 7: [logits], 8: [expo], 9: [make_zs], 12: [group_zs], 14: [quant_zs]}
+
         done = []
-        extra = {0: [e_x], 1: [e_wa], 2: [e_a], 3: [e_logits], 4: [e_exp, e_zs], 5: [e_turn], 6: [e_codes]}
+        full = {}
+
+        def join(k):
+            for f in after.get(k, []):
+                f()
+
+        def put_out(i):
+            for b in full.get(i - DELAY, []):
+                leave(b)
+            full[i] = [b for b in sorted(acc) if b not in done and count[b] == G * (BASE_TIMES + LOW_TIMES)]
+            done.extend(full[i])
 
         widen(0)
         s_inter(0)
-        v_inter_w(0)
+        v_inter_first()
         widen(1)
-        v_inter_b(0)
         for i in range(n):
             t_inter(i + 2)
-            s_inter(i + 1)
             widen(i + 2)
-            quant_w(i)
-            multiply(i, "w_q")
-            v_inter_w(i + 1)
+            s_inter(i + 1)
             quant_b(i)
             multiply(i, "b_q")
-            v_inter_b(i + 1)
-            for f in extra.get(i, []):
-                f()
-            load_b(i + 5)
-            load_w(i + 5)
-            for ci in sorted(full):
-                leave(ci)
-                full.remove(ci)
-            for ci in range(len(CHUNKS)):
-                if ci not in done and (ci, 0) in count and all(count[k] == 20 for k in count if k[0] == ci):
-                    full.append(ci)
-                    done.append(ci)
-        for ci in full:
-            leave(ci)
+            join(3 * i)
+            v_inter(i + 1)
+            join(3 * i + 1)
+            quant_w(i)
+            multiply(i, "w_q")
+            join(3 * i + 2)
+            if i + 5 >= 7:
+                load_b(i + 5)
+                load_w(i + 5)
+            put_out(i)
+        for i in range(n, n + DELAY):
+            put_out(i)

@@ -23,9 +23,9 @@ BANK = 512
 BASE_TIMES = 2
 LOW_TIMES = 3
 DELAY = 2
-STEPS = [(0, 256, [0]), (0, 256, [1]), (0, 256, [2,3]), (256, 512, [0,1]), (256, 512, [2,3]), (768, 1024, [0]), (768, 1024, [1]), (768, 1024, [2]), (768, 1024, [3]), (1792, 1024, [0]), (1792, 1024, [1]), (1792, 1024, [2]), (1792, 1024, [3]), (2816, 1024, [0]), (2816, 1024, [1]), (2816, 1024, [2]), (2816, 1024, [3]), (3840, 128, [0,1,2,3]), (3968, 128, [0,1,2,3])]
-SCALAR_COLS = [0, 0, 0, 0, 0, 0, 208, 208, 208, 208, 208, 208, 208, 208, 208, 208, 464, 224, 224]
-TENSOR_COLS = [0, 0, 0, 0, 256, 256, 256, 256, 256, 256, 256, 256, 256, 256, 256, 256, 0, 0, 0]
+STEPS = [(0, 512, [0]), (0, 512, [1]), (0, 512, [2,3]), (512, 1024, [0]), (512, 1024, [1]), (512, 1024, [2]), (512, 1024, [3]), (1536, 1024, [0]), (1536, 1024, [1]), (1536, 1024, [2]), (1536, 1024, [3]), (2560, 1024, [0]), (2560, 1024, [1]), (2560, 1024, [2]), (2560, 1024, [3]), (3584, 256, [0,1,2,3]), (3840, 128, [0,1,2,3]), (3968, 128, [0,1,2,3])]
+SCALAR_COLS = [0, 0, 0, 432, 432, 432, 368, 112, 112, 112, 112, 112, 112, 112, 112, 336, 304, 304]
+TENSOR_COLS = [0, 0, 0, 0, 0, 0, 0, 256, 256, 256, 256, 256, 256, 256, 256, 256, 0, 0]
 
 
 def tile_hydraloraprototyperouted_w_kernel(tc, x, w0, wa, c, s, wb_bytes, wb_scale, out):
@@ -46,14 +46,14 @@ def tile_hydraloraprototyperouted_w_kernel(tc, x, w0, wa, c, s, wb_bytes, wb_sca
             return w * len(gs)
 
         def size(i):
-            return "wide" if cols(i) > 256 else "narrow"
+            return "wide" if cols(i) > 512 else "half"
 
         def load_w(i):
             if i >= n:
                 return
             n0, w, gs = STEPS[i]
             W = cols(i)
-            t = stream.tile([P, PACK, 2 * W], BF16, name="raw_" + size(i), bufs=4)
+            t = stream.tile([P, PACK, 2 * W], BF16, name="raw_" + size(i), bufs=3)
             for k, g in enumerate(gs):
                 nc.sync.dma_start(out=t[:, :, W + k * w:W + (k + 1) * w], in_=w0[g * 512:(g + 1) * 512, n0:n0 + w].rearrange("(p j) n -> p j n", j=PACK))
             st[i]["raw"] = t
@@ -62,7 +62,7 @@ def tile_hydraloraprototyperouted_w_kernel(tc, x, w0, wa, c, s, wb_bytes, wb_sca
             if i >= n:
                 return
             n0, w, gs = STEPS[i]
-            t = stream.tile([P, PACK, cols(i)], U8, name="b_raw_" + size(i), bufs=4)
+            t = stream.tile([P, PACK, cols(i)], U8, name="b_raw_" + size(i), bufs=4 if cols(i) > 512 else 3)
             for k, g in enumerate(gs):
                 nc.sync.dma_start(out=t[:, :, k * w:(k + 1) * w], in_=wb_bytes[g * 512:(g + 1) * 512, n0:n0 + w].rearrange("(p j) n -> p j n", j=PACK))
             st[i]["b_raw"] = t
@@ -93,7 +93,7 @@ def tile_hydraloraprototyperouted_w_kernel(tc, x, w0, wa, c, s, wb_bytes, wb_sca
             if i >= n:
                 return
             W = cols(i)
-            t = stream.tile([P, 2 * W, PACK], BF16, name="il_" + size(i), bufs=2, align_bytes=64)
+            t = stream.tile([P, 2 * W, PACK], BF16, name="il", bufs=2, align_bytes=64)
             st[i]["il"] = t
             end = 2 * W - TENSOR_COLS[i]
             if end < 2 * W:
@@ -104,12 +104,14 @@ def tile_hydraloraprototyperouted_w_kernel(tc, x, w0, wa, c, s, wb_bytes, wb_sca
         def v_inter(i, c0=0, c1=None):
             if i >= n:
                 return
-            W = cols(i)
-            interleave(nc.vector.tensor_copy, st[i]["il"], st[i]["raw"], c0, 2 * W - TENSOR_COLS[i] - SCALAR_COLS[i] if c1 is None else c1)
+            stop = 2 * cols(i) - TENSOR_COLS[i] - SCALAR_COLS[i]
+            interleave(nc.vector.tensor_copy, st[i]["il"], st[i]["raw"], c0, stop if c1 is None else c1)
 
-        def v_inter_first():
-            v_inter(0, c0=cols(0))
-            v_inter(0, c1=cols(0))
+        def v_inter_w(i):
+            v_inter(i, c0=cols(i))
+
+        def v_inter_b(i):
+            v_inter(i, c1=cols(i))
 
         def quant(i, il, name, bufs):
             q = stream.tile([P, cols(i)], U32, name=name + "_q_" + size(i), bufs=bufs, align_bytes=64)
@@ -118,7 +120,7 @@ def tile_hydraloraprototyperouted_w_kernel(tc, x, w0, wa, c, s, wb_bytes, wb_sca
             return q, z
 
         def quant_w(i):
-            st[i]["w_q"] = quant(i, st[i]["il"][:, cols(i):2 * cols(i), :], "w", 2)
+            st[i]["w_q"] = quant(i, st[i]["il"][:, cols(i):2 * cols(i), :], "w", 3)
 
         def quant_b(i):
             st[i]["b_q"] = quant(i, st[i]["il"][:, 0:cols(i), :], "b", 4)
@@ -165,7 +167,7 @@ def tile_hydraloraprototyperouted_w_kernel(tc, x, w0, wa, c, s, wb_bytes, wb_sca
 
         def leave(b):
             bw = acc[b].shape[1]
-            o = stream.tile([P, bw], F32, name="o", bufs=3)
+            o = stream.tile([P, bw], F32, name="o", bufs=6)
             nc.scalar.activation(out=o[:], in_=acc[b][:], func=ACT.Copy, scale=0.5)
             nc.sync.dma_start(out=out[:, b:b + bw], in_=o[:])
 
@@ -183,7 +185,10 @@ def tile_hydraloraprototyperouted_w_kernel(tc, x, w0, wa, c, s, wb_bytes, wb_sca
         nc.gpsimd.memset(neg_half[:], -0.5)
         x_sb = keep.tile([P, D], BF16, name="rows")
         wa_sb = keep.tile([P, G, PACK, R], BF16)
-        s_bc = keep.tile([P, E * R], BF16)
+        s_row = keep.tile([P, E * R], BF16)
+        nc.vector.memset(s_row[:], 0.0)
+        ones16 = keep.tile([P, P], BF16)
+        nc.gpsimd.memset(ones16[:], 1.0)
         wbs = keep.tile([P, 16], F32)
 
         def load_wbs():
@@ -199,27 +204,26 @@ def tile_hydraloraprototyperouted_w_kernel(tc, x, w0, wa, c, s, wb_bytes, wb_sca
             nc.sync.dma_start(out=c_sb[0:E, :], in_=c)
 
         def load_s():
-            nc.sync.dma_start(out=s_bc[:], in_=s.partition_broadcast(P))
+            nc.sync.dma_start(out=s_row[0:1, :], in_=s.unsqueeze(0))
 
+        load_w(0)
         load_wbs()
         load_b(0)
-        load_w(0)
-        load_b(1)
         load_w(1)
-        load_b(2)
+        load_b(1)
         load_w(2)
         load_x()
+        load_b(2)
         load_wa()
-        load_b(3)
         load_w(3)
+        load_b(3)
         load_c()
-        load_b(4)
         load_w(4)
+        load_b(4)
         load_s()
-        load_b(5)
         load_w(5)
+        load_b(5)
         load_b(6)
-        load_w(6)
 
         def turn(src, name):
             words = src[:].bitcast(F32)
@@ -277,8 +281,8 @@ def tile_hydraloraprototyperouted_w_kernel(tc, x, w0, wa, c, s, wb_bytes, wb_sca
             v["ct_ps"] = ct_ps
 
         def copy_a():
-            v["aT"] = keep.tile([P, P], F32, name="aT")
-            nc.scalar.copy(out=v["aT"][:], in_=v["a"][:, 0, :])
+            v["a_sb"] = keep.tile([P, 2, P], F32, name="a_sb")
+            nc.scalar.copy(out=v["a_sb"][:], in_=v["a"][:])
             v["cT"] = keep.tile([P, E], F32, name="cT")
             nc.scalar.copy(out=v["cT"][:], in_=v["ct_ps"][:, 0:E])
 
@@ -287,9 +291,16 @@ def tile_hydraloraprototyperouted_w_kernel(tc, x, w0, wa, c, s, wb_bytes, wb_sca
             cT2 = keep.tile([P, E], F32)
             nc.vector.tensor_tensor(out=cT2[:], in0=cT[:], in1=cT[:], op=ALU.mult)
             lg = psum.tile([P, E], F32, name="small")
-            nc.tensor.matmul(lg[:], lhsT=v["aT"][:], rhs=cT[:], start=True, stop=False)
+            nc.tensor.matmul(lg[:], lhsT=v["a_sb"][:, 0, :], rhs=cT[:], start=True, stop=False)
             nc.tensor.matmul(lg[:], lhsT=neg_half[:], rhs=cT2[:], start=False, stop=True)
             v["lg"] = lg
+            v["s_bc"] = []
+            for half in range(2):
+                bank = psum.tile([P, 2, BANK], BF16, name="turned", bufs=2)
+                for q in range(2):
+                    c0 = (2 * half + q) * BANK
+                    nc.tensor.matmul(bank[:, q, :], lhsT=ones16[:], rhs=s_row[:, c0:c0 + BANK], start=True, stop=True)
+                v["s_bc"].append(bank)
 
         def expo():
             lg = v["lg"]
@@ -309,7 +320,8 @@ def tile_hydraloraprototyperouted_w_kernel(tc, x, w0, wa, c, s, wb_bytes, wb_sca
             zs = keep.tile([P, E * R], BF16, name="rows")
             for e in range(E):
                 cc = slice(e * R, (e + 1) * R)
-                nc.vector.scalar_tensor_tensor(out=zs[:, cc], in0=v["a"][:, 1, :], scalar=gate[:, e:e + 1], in1=s_bc[:, cc], op0=ALU.mult, op1=ALU.mult)
+                nc.vector.scalar_tensor_tensor(out=zs[:, cc], in0=v["a_sb"][:, 1, :], scalar=gate[:, e:e + 1],
+                                               in1=v["s_bc"][e // 8][:, e // 4 % 2, e % 4 * R:(e % 4 + 1) * R], op0=ALU.mult, op1=ALU.mult)
             v["zs"] = zs
             v["z_b"] = turn(zs, "zs")
 
@@ -319,7 +331,7 @@ def tile_hydraloraprototyperouted_w_kernel(tc, x, w0, wa, c, s, wb_bytes, wb_sca
         def quant_zs():
             arrived("b_q", quant_keep(v["zs_g"], "zs"))
 
-        after = {2: [turn_x, group_x], 5: [inter_wa, quant_x], 6: [mm_a, copy_a], 7: [logits], 8: [expo], 9: [make_zs], 12: [group_zs], 14: [quant_zs]}
+        after = {2: [turn_x], 3: [group_x], 4: [inter_wa, quant_x], 5: [mm_a], 7: [copy_a, logits], 9: [expo], 11: [make_zs], 14: [group_zs, quant_zs]}
 
         done = []
         full = {}
@@ -334,14 +346,48 @@ def tile_hydraloraprototyperouted_w_kernel(tc, x, w0, wa, c, s, wb_bytes, wb_sca
             full[i] = [b for b in sorted(acc) if b not in done and count[b] == G * (BASE_TIMES + LOW_TIMES)]
             done.extend(full[i])
 
-        widen(0)
         s_inter(0)
-        v_inter_first()
+        v_inter_w(0)
+        widen(0)
+        join(0)
+        s_inter(1)
+        quant_w(0)
+        multiply(0, "w_q")
+        v_inter_w(1)
         widen(1)
-        for i in range(n):
-            t_inter(i + 2)
-            widen(i + 2)
+        join(1)
+        v_inter_b(0)
+        quant_w(1)
+        multiply(1, "w_q")
+        quant_b(0)
+        multiply(0, "b_q")
+        join(2)
+        s_inter(2)
+        v_inter_w(2)
+        join(3)
+        widen(2)
+        v_inter_b(1)
+        quant_b(1)
+        multiply(1, "b_q")
+        quant_w(2)
+        multiply(2, "w_q")
+        join(4)
+        s_inter(3)
+        v_inter_w(3)
+        join(5)
+        v_inter_b(2)
+        quant_b(2)
+        multiply(2, "b_q")
+        join(6)
+        widen(3)
+        v_inter_b(3)
+        load_w(6)
+        load_b(7)
+        join(7)
+        for i in range(3, n):
+            widen(i + 1)
             s_inter(i + 1)
+            t_inter(i + 3)
             quant_b(i)
             multiply(i, "b_q")
             join(3 * i)
@@ -350,9 +396,8 @@ def tile_hydraloraprototyperouted_w_kernel(tc, x, w0, wa, c, s, wb_bytes, wb_sca
             quant_w(i)
             multiply(i, "w_q")
             join(3 * i + 2)
-            if i + 5 >= 7:
-                load_b(i + 5)
-                load_w(i + 5)
+            load_b(i + 5)
+            load_w(i + 4)
             put_out(i)
         for i in range(n, n + DELAY):
             put_out(i)

from contextlib import ExitStack

import concourse.mybir as mybir
from concourse.masks import make_identity

T, D, F, R, E = 128, 2048, 4096, 128, 16
FLOPS = 2 * T * D * F * 2 + 2 * T * D * R

F32 = mybir.dt.float32
BF16 = mybir.dt.bfloat16
U32 = mybir.dt.uint32
U8 = mybir.dt.uint8
F8 = mybir.dt.float8_e4m3fn
X4 = mybir.dt.float8_e4m3fn_x4
ACT = mybir.ActivationFunctionType
ALU = mybir.AluOpType
AX = mybir.AxisListType

P = 128
PACK = 4
G = 4
BANK = 512
BASE_TIMES = 2
LOW_TIMES = 3
DELAY = 2
STEPS = [(0, 512, [0]), (0, 512, [1]), (0, 512, [2,3]), (512, 1024, [0]), (512, 1024, [1]), (512, 1024, [2]), (512, 1024, [3]), (1536, 1024, [0]), (1536, 1024, [1]), (1536, 1024, [2]), (1536, 1024, [3]), (2560, 1024, [0]), (2560, 1024, [1]), (2560, 1024, [2]), (2560, 1024, [3]), (3584, 256, [0,1,2,3]), (3840, 128, [0,1,2,3]), (3968, 128, [0,1,2,3])]
SCALAR_COLS = [0, 0, 0, 432, 432, 432, 368, 112, 112, 112, 112, 112, 112, 112, 112, 336, 304, 304]
TENSOR_COLS = [0, 0, 0, 0, 0, 0, 0, 256, 256, 256, 256, 256, 256, 256, 256, 256, 0, 0]


def tile_hydraloraprototyperouted_w_kernel(tc, x, w0, wa, c, s, wb_bytes, wb_scale, out):
    nc = tc.nc
    with ExitStack() as ctx:
        keep = ctx.enter_context(tc.tile_pool(name="keep", bufs=1))
        stream = ctx.enter_context(tc.tile_pool(name="stream", bufs=3))
        psum = ctx.enter_context(tc.psum_pool(name="psum", bufs=1))
        ctx.enter_context(tc.manual_schedule())

        n = len(STEPS)
        st = [dict() for i in range(n)]
        acc = {}
        count = {}

        def cols(i):
            n0, w, gs = STEPS[i]
            return w * len(gs)

        def size(i):
            return "wide" if cols(i) > 512 else "half"

        def load_w(i):
            if i >= n:
                return
            n0, w, gs = STEPS[i]
            W = cols(i)
            t = stream.tile([P, PACK, 2 * W], BF16, name="raw_" + size(i), bufs=3)
            for k, g in enumerate(gs):
                nc.sync.dma_start(out=t[:, :, W + k * w:W + (k + 1) * w], in_=w0[g * 512:(g + 1) * 512, n0:n0 + w].rearrange("(p j) n -> p j n", j=PACK))
            st[i]["raw"] = t

        def load_b(i):
            if i >= n:
                return
            n0, w, gs = STEPS[i]
            t = stream.tile([P, PACK, cols(i)], U8, name="b_raw_" + size(i), bufs=4 if cols(i) > 512 else 3)
            for k, g in enumerate(gs):
                nc.sync.dma_start(out=t[:, :, k * w:(k + 1) * w], in_=wb_bytes[g * 512:(g + 1) * 512, n0:n0 + w].rearrange("(p j) n -> p j n", j=PACK))
            st[i]["b_raw"] = t

        def widen(i):
            if i >= n:
                return
            n0, w, gs = STEPS[i]
            t = st[i]["raw"]
            for k, g in enumerate(gs):
                for j in range(PACK):
                    nc.scalar.activation(out=t[:, j, k * w:(k + 1) * w], in_=st[i]["b_raw"][:, j, k * w:(k + 1) * w].bitcast(F8), func=ACT.Copy, scale=wbs[:, 4 * g + j:4 * g + j + 1])

        def interleave(copy, dst, src, c0, c1):
            copy(out=dst[:, c0:c1, :].rearrange("p (c i) t -> p c t i", i=4), in_=src[:, :, c0:c1].rearrange("p t (c i) -> p c t i", i=4))

        def t_inter(i):
            if i >= n or TENSOR_COLS[i] == 0:
                return
            W = cols(i)
            bank = psum.tile([P, TENSOR_COLS[i], PACK], BF16, name="turned", bufs=2)
            for h in range(TENSOR_COLS[i] // P):
                c0 = 2 * W - TENSOR_COLS[i] + h * P
                nc.tensor.matmul(bank[:, h * P:(h + 1) * P, :].rearrange("p n j -> p (n j)"), lhsT=ident16[:], rhs=st[i]["raw"][:, :, c0:c0 + P].rearrange("p j n -> p n j"), start=True, stop=True)
            st[i]["bank"] = bank

        def s_inter(i):
            if i >= n:
                return
            W = cols(i)
            t = stream.tile([P, 2 * W, PACK], BF16, name="il", bufs=2, align_bytes=64)
            st[i]["il"] = t
            end = 2 * W - TENSOR_COLS[i]
            if end < 2 * W:
                nc.scalar.copy(out=t[:, end:2 * W, :].rearrange("p w t -> p (w t)"), in_=st[i]["bank"][:].rearrange("p n j -> p (n j)"))
            if SCALAR_COLS[i] > 0:
                interleave(nc.scalar.copy, t, st[i]["raw"], end - SCALAR_COLS[i], end)

        def v_inter(i, c0=0, c1=None):
            if i >= n:
                return
            stop = 2 * cols(i) - TENSOR_COLS[i] - SCALAR_COLS[i]
            interleave(nc.vector.tensor_copy, st[i]["il"], st[i]["raw"], c0, stop if c1 is None else c1)

        def v_inter_w(i):
            v_inter(i, c0=cols(i))

        def v_inter_b(i):
            v_inter(i, c1=cols(i))

        def quant(i, il, name, bufs):
            q = stream.tile([P, cols(i)], U32, name=name + "_q_" + size(i), bufs=bufs, align_bytes=64)
            z = stream.tile([P, cols(i)], U8, name=name + "_z_" + size(i), bufs=bufs, align_bytes=64)
            nc.vector.quantize_mx(out=q[:].bitcast(X4), scales=z[:], in_=il.rearrange("p w t -> p (w t)"))
            return q, z

        def quant_w(i):
            st[i]["w_q"] = quant(i, st[i]["il"][:, cols(i):2 * cols(i), :], "w", 3)

        def quant_b(i):
            st[i]["b_q"] = quant(i, st[i]["il"][:, 0:cols(i), :], "b", 4)

        def mm(i, key):
            times = BASE_TIMES if key == "w_q" else LOW_TIMES
            n0, w, gs = STEPS[i]
            q, z = st[i][key]
            lq, lz = left[key]
            bw = min(w, BANK)
            for k, g in enumerate(gs):
                for h in range(w // bw):
                    b = n0 + h * bw
                    if b not in acc:
                        acc[b] = psum.tile([P, bw], F32, name="acc", bufs=4)
                        count[b] = 0
                    for r in range(times):
                        count[b] += 1
                        nc.tensor.matmul_mx(
                            out=acc[b][:],
                            lhsT=lq[:, g * P:(g + 1) * P].bitcast(X4),
                            lhsT_scale=lz[:, g * P:(g + 1) * P],
                            rhs=q[:, k * w + h * bw:k * w + (h + 1) * bw].bitcast(X4),
                            rhs_scale=z[:, k * w + h * bw:k * w + (h + 1) * bw],
                            start=(count[b] == 1),
                            stop=(count[b] == G * (BASE_TIMES + LOW_TIMES)),
                        )

        waiting = {"w_q": [], "b_q": []}
        left = {}

        def multiply(i, key):
            waiting[key].append(i)
            if key in left:
                for k in waiting[key]:
                    mm(k, key)
                waiting[key].clear()

        def arrived(key, codes):
            left[key] = codes
            for k in waiting[key]:
                mm(k, key)
            waiting[key].clear()

        def leave(b):
            bw = acc[b].shape[1]
            o = stream.tile([P, bw], F32, name="o", bufs=6)
            nc.scalar.activation(out=o[:], in_=acc[b][:], func=ACT.Copy, scale=0.5)
            nc.sync.dma_start(out=out[:, b:b + bw], in_=o[:])

        one = keep.tile([P, 1], F32)
        nc.vector.memset(one[:], 1.0)
        warm = keep.tile([P, 1], F32)
        nc.scalar.activation(out=warm[:], in_=one[:], func=ACT.Exp)
        ident = keep.tile([P, P], F32)
        make_identity(nc, ident[:])
        ident16 = keep.tile([P, P], BF16)
        nc.gpsimd.tensor_copy(out=ident16[:], in_=ident[:])
        c_sb = keep.tile([P, P], BF16)
        nc.gpsimd.memset(c_sb[:], 0.0)
        neg_half = keep.tile([P, P], F32)
        nc.gpsimd.memset(neg_half[:], -0.5)
        x_sb = keep.tile([P, D], BF16, name="rows")
        wa_sb = keep.tile([P, G, PACK, R], BF16)
        s_row = keep.tile([P, E * R], BF16)
        nc.vector.memset(s_row[:], 0.0)
        ones16 = keep.tile([P, P], BF16)
        nc.gpsimd.memset(ones16[:], 1.0)
        wbs = keep.tile([P, 16], F32)

        def load_wbs():
            nc.sync.dma_start(out=wbs[:].rearrange("p (g t) -> p g t", t=4), in_=wb_scale.rearrange("(g p t) o -> p g (t o)", p=P, t=4))

        def load_x():
            nc.sync.dma_start(out=x_sb[:], in_=x)

        def load_wa():
            nc.sync.dma_start(out=wa_sb[:], in_=wa.rearrange("(g p j) r -> p g j r", p=P, j=PACK))

        def load_c():
            nc.sync.dma_start(out=c_sb[0:E, :], in_=c)

        def load_s():
            nc.sync.dma_start(out=s_row[0:1, :], in_=s.unsqueeze(0))

        load_w(0)
        load_wbs()
        load_b(0)
        load_w(1)
        load_b(1)
        load_w(2)
        load_x()
        load_b(2)
        load_wa()
        load_w(3)
        load_b(3)
        load_c()
        load_w(4)
        load_b(4)
        load_s()
        load_w(5)
        load_b(5)
        load_b(6)

        def turn(src, name):
            words = src[:].bitcast(F32)
            banks = []
            for half in range(2):
                bank = psum.tile([P, 2, 2, P], F32, name="turned", bufs=2)
                for gg in range(2):
                    g = 2 * half + gg
                    for u in range(2):
                        nc.tensor.transpose(bank[:, gg, u, :], words[:, 256 * g + u:256 * (g + 1):2], ident[:])
                banks.append(bank)
            return banks

        def group(banks, name, copy):
            grouped = keep.tile([P, G, P, PACK], BF16, name="rows_g", align_bytes=64)
            for half in range(2):
                view = grouped[:, 2 * half:2 * half + 2, :, :].rearrange("p g r t -> p g (r t)").bitcast(F32).rearrange("p g (r u) -> p g r u", u=2)
                copy(out=view, in_=banks[half][:].rearrange("p g u r -> p g r u"))
            return grouped

        def quant_keep(grouped, name):
            q = keep.tile([P, 512], U32, name=name + "_q", align_bytes=64)
            z = keep.tile([P, 512], U8, name=name + "_z", align_bytes=64)
            nc.vector.quantize_mx(out=q[:].bitcast(X4), scales=z[:], in_=grouped[:].rearrange("p g r t -> p (g r t)"))
            return q, z

        v = {}

        def turn_x():
            v["x_b"] = turn(x_sb, "x")

        def group_x():
            v["x_g"] = group(v["x_b"], "x", nc.scalar.copy)

        def inter_wa():
            v["wa_g"] = keep.tile([P, G, R, PACK], BF16, name="wa_g", align_bytes=64)
            nc.vector.tensor_copy(out=v["wa_g"][:], in_=wa_sb[:].rearrange("p g j r -> p g r j"))

        def quant_x():
            v["x"] = quant_keep(v["x_g"], "x")
            arrived("w_q", v["x"])

        def mm_a():
            v["wa"] = quant_keep(v["wa_g"], "wa")
            a_ps = psum.tile([P, 2, P], F32, name="a_ps")
            v["a"] = a_ps
            for side in range(2):
                for g in range(G):
                    cc = slice(g * P, (g + 1) * P)
                    l, r = (v["wa"], v["x"]) if side == 0 else (v["x"], v["wa"])
                    nc.tensor.matmul_mx(out=a_ps[:, side, :], lhsT=l[0][:, cc].bitcast(X4), lhsT_scale=l[1][:, cc],
                                        rhs=r[0][:, cc].bitcast(X4), rhs_scale=r[1][:, cc], start=(g == 0), stop=(g == G - 1))
            ct_ps = psum.tile([P, P], BF16, name="small")
            nc.tensor.transpose(ct_ps[:], c_sb[:], ident16[:])
            v["ct_ps"] = ct_ps

        def copy_a():
            v["a_sb"] = keep.tile([P, 2, P], F32, name="a_sb")
            nc.scalar.copy(out=v["a_sb"][:], in_=v["a"][:])
            v["cT"] = keep.tile([P, E], F32, name="cT")
            nc.scalar.copy(out=v["cT"][:], in_=v["ct_ps"][:, 0:E])

        def logits():
            cT = v["cT"]
            cT2 = keep.tile([P, E], F32)
            nc.vector.tensor_tensor(out=cT2[:], in0=cT[:], in1=cT[:], op=ALU.mult)
            lg = psum.tile([P, E], F32, name="small")
            nc.tensor.matmul(lg[:], lhsT=v["a_sb"][:, 0, :], rhs=cT[:], start=True, stop=False)
            nc.tensor.matmul(lg[:], lhsT=neg_half[:], rhs=cT2[:], start=False, stop=True)
            v["lg"] = lg
            v["s_bc"] = []
            for half in range(2):
                bank = psum.tile([P, 2, BANK], BF16, name="turned", bufs=2)
                for q in range(2):
                    c0 = (2 * half + q) * BANK
                    nc.tensor.matmul(bank[:, q, :], lhsT=ones16[:], rhs=s_row[:, c0:c0 + BANK], start=True, stop=True)
                v["s_bc"].append(bank)

        def expo():
            lg = v["lg"]
            top = keep.tile([P, 1], F32)
            nc.vector.reduce_max(out=top[:], in_=lg[:], axis=AX.X)
            ntop = keep.tile([P, 1], F32)
            nc.vector.tensor_scalar(out=ntop[:], in0=top[:], scalar1=-0.125, scalar2=None, op0=ALU.mult)
            v["ex"] = keep.tile([P, E], F32, name="ex")
            v["total"] = keep.tile([P, 1], F32, name="total")
            nc.scalar.activation(out=v["ex"][:], in_=lg[:], func=ACT.Exp, bias=ntop[:], scale=0.125, accum_out=v["total"][:])

        def make_zs():
            inv = keep.tile([P, 1], F32)
            nc.vector.reciprocal(out=inv[:], in_=v["total"][:])
            gate = keep.tile([P, E], F32)
            nc.vector.tensor_scalar(out=gate[:], in0=v["ex"][:], scalar1=inv[:], scalar2=None, op0=ALU.mult)
            zs = keep.tile([P, E * R], BF16, name="rows")
            for e in range(E):
                cc = slice(e * R, (e + 1) * R)
                nc.vector.scalar_tensor_tensor(out=zs[:, cc], in0=v["a_sb"][:, 1, :], scalar=gate[:, e:e + 1],
                                               in1=v["s_bc"][e // 8][:, e // 4 % 2, e % 4 * R:(e % 4 + 1) * R], op0=ALU.mult, op1=ALU.mult)
            v["zs"] = zs
            v["z_b"] = turn(zs, "zs")

        def group_zs():
            v["zs_g"] = group(v["z_b"], "zs", nc.scalar.copy)

        def quant_zs():
            arrived("b_q", quant_keep(v["zs_g"], "zs"))

        after = {2: [turn_x], 3: [group_x], 4: [inter_wa, quant_x], 5: [mm_a], 7: [copy_a, logits], 9: [expo], 11: [make_zs], 14: [group_zs, quant_zs]}

        done = []
        full = {}

        def join(k):
            for f in after.get(k, []):
                f()

        def put_out(i):
            for b in full.get(i - DELAY, []):
                leave(b)
            full[i] = [b for b in sorted(acc) if b not in done and count[b] == G * (BASE_TIMES + LOW_TIMES)]
            done.extend(full[i])

        s_inter(0)
        v_inter_w(0)
        widen(0)
        join(0)
        s_inter(1)
        quant_w(0)
        multiply(0, "w_q")
        v_inter_w(1)
        widen(1)
        join(1)
        v_inter_b(0)
        quant_w(1)
        multiply(1, "w_q")
        quant_b(0)
        multiply(0, "b_q")
        join(2)
        s_inter(2)
        v_inter_w(2)
        join(3)
        widen(2)
        v_inter_b(1)
        quant_b(1)
        multiply(1, "b_q")
        quant_w(2)
        multiply(2, "w_q")
        join(4)
        s_inter(3)
        v_inter_w(3)
        join(5)
        v_inter_b(2)
        quant_b(2)
        multiply(2, "b_q")
        join(6)
        widen(3)
        v_inter_b(3)
        load_w(6)
        load_b(7)
        join(7)
        for i in range(3, n):
            widen(i + 1)
            s_inter(i + 1)
            t_inter(i + 3)
            quant_b(i)
            multiply(i, "b_q")
            join(3 * i)
            v_inter(i + 1)
            join(3 * i + 1)
            quant_w(i)
            multiply(i, "w_q")
            join(3 * i + 2)
            load_b(i + 5)
            load_w(i + 4)
            put_out(i)
        for i in range(n, n + DELAY):
            put_out(i)
